import numpy as np
import ml_dtypes


def mxq(x, axis, fmt="e4m3"):
    dtype, down = {"e4m3": (ml_dtypes.float8_e4m3fn, 7), "e5m2": (ml_dtypes.float8_e5m2, 14)}[fmt]
    v = np.moveaxis(np.asarray(x, np.float32).astype(ml_dtypes.bfloat16).astype(np.float64), axis, -1)
    blocks = v.reshape(v.shape[:-1] + (-1, 32))
    amax = np.abs(blocks).max(-1, keepdims=True)
    byte = np.maximum(np.where(amax > 0, np.frexp(amax)[1] - 1 + 127, 0) - down, 1)
    scale = np.exp2(byte - 127.0)
    codes = (blocks / scale).astype(np.float32).astype(dtype).astype(np.float64)
    return np.moveaxis((codes * scale).reshape(v.shape), -1, axis)


WIDE = False


def mx_kscale(k):
    if not WIDE:
        return np.ones(k)
    levels = np.array([30, -30])
    if k % 512:
        return np.exp2(np.random.permutation(np.resize(levels, k // 32))).repeat(32)
    a = np.empty((k // 512, 16))
    for p in range(k // 512):
        a[p, :8] = np.random.permutation(np.resize(levels, 8))
        for g in range(8):
            far = levels[np.abs(levels - a[p, g]) >= 10]
            a[p, g + 8] = far[np.random.randint(len(far))]
    return np.exp2(a.ravel()).repeat(32)


BF16 = ml_dtypes.bfloat16


def bf(x):
    return np.asarray(x, np.float32).astype(BF16)


def f64(x):
    return np.asarray(x).astype(np.float64)


E2M1 = np.array([0.0, 0.5, 1.0, 1.5, 2.0, 3.0, 4.0, 6.0, -0.0, -0.5, -1.0, -1.5, -2.0, -3.0, -4.0, -6.0])


def pack_weight(w, fmt):
    k, n = w.shape
    w = f64(bf(w)).reshape(k // 32, 32, n)
    amax = np.abs(w).max(1)
    if fmt in ("e4m3", "e5m2"):
        byte = np.frexp(amax)[1] - 1 + 127 - (7 if fmt == "e4m3" else 14)
    else:
        mant, ex = np.frexp(amax / 6.0)
        byte = np.where(mant > 0.5, ex, ex - 1) + 127
    byte = np.clip(np.where(amax > 0, byte, 1), 1, 254)
    scaled = (w * np.exp2(127.0 - byte)[:, None, :]).reshape(k, n).astype(np.float32)
    by_word = np.ascontiguousarray(scaled.reshape(k // 512, 128, 4, n).transpose(0, 1, 3, 2))
    if fmt in ("e4m3", "e5m2"):
        words = by_word.astype(ml_dtypes.float8_e4m3fn if fmt == "e4m3" else ml_dtypes.float8_e5m2).view(np.uint8)
    else:
        c = by_word.astype(ml_dtypes.float4_e2m1fn).view(np.uint8) & 0xF
        words = c[..., 0::2] | (c[..., 1::2] << 4)
    return np.ascontiguousarray(words), np.ascontiguousarray(byte.astype(np.uint8).reshape(k // 512, 16, n))


def unpack_weight(words, scales, fmt):
    g, p, n, _ = words.shape
    if fmt in ("e4m3", "e5m2"):
        vals = np.ascontiguousarray(words).view(ml_dtypes.float8_e4m3fn if fmt == "e4m3" else ml_dtypes.float8_e5m2).astype(np.float64)
    else:
        nib = np.empty((g, p, n, 4), np.uint8)
        nib[..., 0::2] = words & 0xF
        nib[..., 1::2] = words >> 4
        vals = E2M1[nib]
    vals = vals * np.repeat(np.exp2(scales.astype(np.float64) - 127.0), 8, axis=1)[..., None]
    return vals.transpose(0, 1, 3, 2).reshape(g * 512, n)


NX, NU, NP, H = 1024, 512, 1024, 1536


def setup_inputs():
    s, t = mx_kscale(NX), mx_kscale(H)
    G = np.random.standard_normal((NX, NP)) * np.exp(0.5 * np.random.standard_normal((NX, NP)))
    g_words, g_scales = pack_weight(G * s[:, None], "e5m2")
    z = np.random.standard_normal(H)
    return {"g_words": g_words, "g_scales": g_scales,
            "w2": bf(np.random.standard_normal((NX, H)) / np.sqrt(NX) / s[:, None] * t),
            "d": bf(1 - np.tanh(z) ** 2),
            "wx": bf(np.random.standard_normal((H, NX)) / np.sqrt(H) / t[:, None]),
            "wu": bf(np.random.standard_normal((H, NU)) / np.sqrt(H) / t[:, None]),
            "lx": bf(0.5 * np.random.standard_normal((NP, NX))),
            "lu": bf(0.5 * np.random.standard_normal((NP, NU)))}


def reference(g_words, g_scales, w2, d, wx, wu, lx, lu):
    G = unpack_weight(g_words, g_scales, "e5m2")
    y = G.T @ mxq(f64(w2), 0, "e4m3")
    y = y * f64(d)
    yq = mxq(y, 1, "e5m2")
    q_x = (yq @ mxq(f64(wx), 0, "e4m3")) + f64(lx)
    q_u = (yq @ mxq(f64(wu), 0, "e4m3")) + f64(lu)
    return q_x, q_u

@@ -1,0 +1,274 @@
+from contextlib import ExitStack
+
+import concourse.mybir as mybir
+
+F32 = mybir.dt.float32
+BF16 = mybir.dt.bfloat16
+I32 = mybir.dt.int32
+U32 = mybir.dt.uint32
+U8 = mybir.dt.uint8
+E4 = mybir.dt.float8_e4m3fn_x4
+E5 = mybir.dt.float8_e5m2_x4
+COPY = mybir.ActivationFunctionType.Copy
+ADD = mybir.AluOpType.add
+MULT = mybir.AluOpType.mult
+
+NX, NU, NP, H = 1024, 512, 1024, 1536
+P = 128
+FLOPS = 2 * NP * NX * H + 2 * NP * H * (NX + NU)
+
+PLAN = [["w2",1,0,512],
+    ["w2",0,0,256],
+    ["w2",0,1,64],
+    ["m1",0,0],
+    ["m1",0,1],
+    ["w2",1,1,512],
+    ["ev",0,0,1],
+    ["w2",0,2,256],
+    ["w2",1,2,320],
+    ["m1",1,0],
+    ["ev",0,1,1],
+    ["yI",0,0,512],
+    ["wI",0,1,512],
+    ["m1",1,1],
+    ["ev",1,0,0],
+    ["wI",0,0,384],
+    ["m1",2,0],
+    ["yI",1,0,384],
+    ["ev",1,1,0],
+    ["wI",1,0,512],
+    ["m1",2,1],
+    ["wI",1,1,512],
+    ["ev",2,0,0],
+    ["wI",2,1,0],
+    ["yI",2,0,384],
+    ["ev",2,1,0],
+    ["m2p",0,1,0],
+    ["wI",2,0,512],
+    ["m2p",0,1,1],
+    ["yI",2,1,256],
+    ["m2p",0,1,2],
+    ["o",1,1,0],
+    ["o",3,1,0],
+    ["yI",0,1,0],
+    ["yI",1,1,128],
+    ["m2p",0,0,0],
+    ["m2p",0,0,1],
+    ["m2p",0,0,2],
+    ["o",0,1,0],
+    ["o",2,1,0],
+    ["m2p",1,0,0],
+    ["wI",0,2,0],
+    ["o",2,0,0],
+    ["m2p",1,0,1],
+    ["m2p",1,0,2],
+    ["o",3,0,0],
+    ["o",0,0,0],
+    ["o",1,0,0],
+    ["o",5,0,0],
+    ["m2p",1,1,0],
+    ["o",7,0,0],
+    ["wI",1,2,0],
+    ["m2p",1,1,1],
+    ["m2p",1,1,2],
+    ["o",4,0,0],
+    ["o",6,0,0],
+    ["o",4,1,0],
+    ["wI",2,2,128],
+    ["m2p",1,2,0],
+    ["f"],
+    ["o",6,1,0],
+    ["m2p",1,2,1],
+    ["o",5,1,0],
+    ["m2p",1,2,2],
+    ["o",7,1,0],
+    ["m2p",0,2,0],
+    ["o",4,2,0],
+    ["o",7,2,0],
+    ["o",5,2,0],
+    ["o",6,2,0],
+    ["m2p",0,2,1],
+    ["m2p",0,2,2],
+    ["o",0,2,0],
+    ["o",1,2,0],
+    ["o",3,2,0],
+    ["o",2,2,0]]
+
+
+def tile_mixed_hessian_jacobian_e3_kernel(tc, g_words, g_scales, w2, d, wx, wu, lx, lu, q_x, q_u):
+    nc = tc.nc
+    with ExitStack() as ctx:
+        ctx.enter_context(tc.manual_schedule())
+        keep = ctx.enter_context(tc.tile_pool(name="keep", bufs=1))
+        ipool = ctx.enter_context(tc.tile_pool(name="ipool", bufs=8))
+        ypool = ctx.enter_context(tc.tile_pool(name="ypool", bufs=6))
+        opool = ctx.enter_context(tc.tile_pool(name="opool", bufs=8))
+        psum = ctx.enter_context(tc.psum_pool(name="psum", bufs=8))
+
+        g_sc = keep.tile([P, 2, NP], U8, align_bytes=64, name="g_sc")
+        nc.gpsimd.memset(g_sc[:].rearrange("p g n -> p (g n)").bitcast(I32), 0)
+        d_raw = keep.tile([P, 3, 4], BF16, align_bytes=64, name="d_raw")
+        nc.scalar.dma_start(out=d_raw[:], in_=d.rearrange("(h p t) -> p h t", p=P, t=4))
+        d_col = keep.tile([P, 12], F32, align_bytes=64, name="d_col")
+
+        w2_raw = {}
+        for hc in range(3):
+            for g in range(2):
+                w2_raw[g, hc] = keep.tile([P, 4, 512], BF16, align_bytes=64, name="w2r%d%d" % (g, hc))
+        g_cod = [keep.tile([P, 2, 512], U32, align_bytes=64, name="gc%d" % ph) for ph in range(2)]
+
+        def load_w2(g, hc, a, b):
+            src = w2[512 * g : 512 * (g + 1), 512 * hc + a : 512 * hc + b]
+            nc.sync.dma_start(out=w2_raw[g, hc][:, :, a:b], in_=src.rearrange("(p j) c -> p j c", j=4))
+
+        def load_g(ph):
+            src = g_words.rearrange("g p n t -> p g (n t)")[:, :, 2048 * ph : 2048 * (ph + 1)]
+            nc.sync.dma_start(out=g_cod[ph][:].bitcast(I32), in_=src.bitcast(I32))
+
+        for g in range(2):
+            for half in range(2):
+                load_w2(g, 0, 256 * half, 256 * (half + 1))
+        for q in range(4):
+            nc.sync.dma_start(
+                out=g_sc[32 * q : 32 * q + 4, :, :].bitcast(I32),
+                in_=g_scales[:, 4 * q : 4 * q + 4, :].rearrange("g r n -> r g n").bitcast(I32),
+            )
+        load_g(0)
+        load_w2(0, 1, 0, 512)
+        load_w2(1, 1, 0, 512)
+        load_g(1)
+        load_w2(0, 2, 0, 512)
+        load_w2(1, 2, 0, 512)
+        wx_raw = []
+        wu_raw = []
+        for hc in range(3):
+            t = keep.tile([P, 4, NX], BF16, align_bytes=64, name="wxr%d" % hc)
+            nc.sync.dma_start(out=t[:], in_=wx[512 * hc : 512 * (hc + 1), :].rearrange("(p j) c -> p j c", j=4))
+            wx_raw.append(t)
+        lxt = []
+        for ph in range(2):
+            lxt.append(keep.tile([P, 4, NX], BF16, align_bytes=64, name="lx%d" % ph))
+        lut = keep.tile([P, 8, NU], BF16, align_bytes=64, name="lut")
+
+        def load_lx(ph):
+            nc.sync.dma_start(out=lxt[ph][:], in_=lx[512 * ph : 512 * (ph + 1), :].rearrange("(a p) n -> p a n", p=P))
+
+        load_lx(0)
+        for hc in range(3):
+            t = keep.tile([P, 4, NU], BF16, align_bytes=64, name="wur%d" % hc)
+            nc.sync.dma_start(out=t[:], in_=wu[512 * hc : 512 * (hc + 1), :].rearrange("(p j) c -> p j c", j=4))
+            wu_raw.append(t)
+        load_lx(1)
+        nc.sync.dma_start(out=lut[:], in_=lu.rearrange("(a p) n -> p a n", p=P))
+
+        nc.scalar.activation(out=d_col[:], in_=d_raw[:].rearrange("p h t -> p (h t)"), func=COPY)
+
+        codes = {}
+        planes = {}
+        pending = []
+
+        def flush():
+            while pending:
+                key, tile_in, fmt = pending.pop(0)
+                c = keep.tile([P, 512], U32, align_bytes=64, name="c" + "".join(str(k) for k in key))
+                s = keep.tile([P, 512], U8, align_bytes=64, name="s" + "".join(str(k) for k in key))
+                nc.vector.quantize_mx(out=c[:].bitcast(fmt), scales=s[:], in_=tile_in[:])
+                codes[key] = c
+                planes[key] = s
+
+        def inter(dst, src, a, b, on_v):
+            o = dst[:, 4 * a : 4 * b].rearrange("p (c i t) -> p c t i", i=4, t=4)
+            i = src[:, :, a:b].rearrange("p t (c i) -> p c t i", i=4)
+            if on_v:
+                nc.vector.tensor_copy(out=o, in_=i)
+            else:
+                nc.scalar.copy(out=o, in_=i)
+
+        def inter_perm(dst, src, a, b, on_v):
+            o = dst[:].rearrange("p (t m j) -> p m j t", t=4, j=4)[:, a // 4 : b // 4]
+            i = src[:, :, a:b].rearrange("p j (m t) -> p m j t", t=4)
+            if on_v:
+                nc.vector.tensor_copy(out=o, in_=i)
+            else:
+                nc.scalar.copy(out=o, in_=i)
+
+        def unit(key, src, v, fn, fmt, cuts=(0, 512)):
+            dst = ipool.tile([P, 2048], BF16, align_bytes=64, name="inter")
+            first = True
+            for a, b in zip(cuts[:-1], cuts[1:]):
+                m = a + v * (b - a) // 512
+                if m > a:
+                    fn(dst, src, a, m, True)
+                if first:
+                    flush()
+                    first = False
+                if m < b:
+                    fn(dst, src, m, b, False)
+            pending.append((key, dst, fmt))
+
+        acc1 = {}
+        acc2 = {}
+        ytiles = {}
+        for step in PLAN:
+            kind = step[0]
+            if kind == "w2":
+                g, hc, v = step[1:]
+                unit(("w2", g, hc), w2_raw[g, hc], v, inter_perm, E4, (0, 256, 512) if hc == 0 else (0, 512))
+            elif kind == "wI":
+                hc, c, v = step[1:]
+                src = wx_raw[hc][:, :, 512 * c : 512 * (c + 1)] if c < 2 else wu_raw[hc][:]
+                unit(("wx", hc, c), src, v, inter, E4)
+            elif kind == "m1":
+                hc, ph = step[1:]
+                for t in range(4):
+                    acc = psum.tile([P, 512], F32, name="acc")
+                    acc1[hc, ph, t] = acc
+                    for g in range(2):
+                        nc.tensor.matmul_mx(
+                            out=acc[:],
+                            lhsT=codes["w2", g, hc][:, 128 * t : 128 * (t + 1)].bitcast(E4),
+                            lhsT_scale=planes["w2", g, hc][:, 128 * t : 128 * (t + 1)],
+                            rhs=g_cod[ph][:, g, :].bitcast(E5),
+                            rhs_scale=g_sc[:, g, 512 * ph : 512 * (ph + 1)],
+                            start=(g == 0),
+                            stop=(g == 1),
+                        )
+            elif kind == "ev":
+                hc, ph, nv = step[1:]
+                y = ypool.tile([P, 4, 512], BF16, align_bytes=64, name="y")
+                ytiles[hc, ph] = y
+                for t in range(4):
+                    dc = d_col[:, 4 * hc + t : 4 * hc + t + 1]
+                    acc = acc1[hc, ph, t]
+                    if t >= 4 - nv:
+                        nc.vector.tensor_scalar(out=y[:, t, :], in0=acc[:], scalar1=dc, scalar2=None, op0=MULT)
+                    else:
+                        nc.scalar.activation(out=y[:, t, :], in_=acc[:], func=COPY, scale=dc)
+            elif kind == "yI":
+                hc, ph, v = step[1:]
+                unit(("y", hc, ph), ytiles[hc, ph], v, inter, E5)
+            elif kind == "m2p":
+                ph, c, hc = step[1:]
+                for pt in range(4 * ph, 4 * ph + 4):
+                    if hc == 0:
+                        acc2[pt, c] = psum.tile([P, 512], F32, name="acc")
+                    cols = slice(128 * (pt % 4), 128 * (pt % 4 + 1))
+                    nc.tensor.matmul_mx(
+                        out=acc2[pt, c][:],
+                        lhsT=codes["y", hc, ph][:, cols].bitcast(E5),
+                        lhsT_scale=planes["y", hc, ph][:, cols],
+                        rhs=codes["wx", hc, c][:].bitcast(E4),
+                        rhs_scale=planes["wx", hc, c][:],
+                        start=(hc == 0),
+                        stop=(hc == 2),
+                    )
+            elif kind == "o":
+                pt, c = step[1:3]
+                o = opool.tile([P, 512], F32, align_bytes=64, name="o")
+                add = lxt[pt // 4][:, pt % 4, 512 * c : 512 * (c + 1)] if c < 2 else lut[:, pt, :]
+                nc.vector.tensor_tensor(out=o[:], in0=acc2[pt, c][:], in1=add, op=ADD)
+                rows = slice(P * pt, P * (pt + 1))
+                dst = q_x[rows, 512 * c : 512 * (c + 1)] if c < 2 else q_u[rows, :]
+                nc.sync.dma_start(out=dst, in_=o[:])
+            else:
+                flush()

@@ -17,82 +17,84 @@ NX, NU, NP, H = 1024, 512, 1024, 1536
 P = 128
 FLOPS = 2 * NP * NX * H + 2 * NP * H * (NX + NU)
 
-PLAN = [["w2",1,0,512],
-    ["w2",0,0,256],
-    ["w2",0,1,64],
-    ["m1",0,0],
-    ["m1",0,1],
-    ["w2",1,1,512],
-    ["ev",0,0,1],
-    ["w2",0,2,256],
-    ["w2",1,2,320],
-    ["m1",1,0],
-    ["ev",0,1,1],
+PLAN = [["w2",0,0,128],
+    ["w2",1,0,512],
+    ["m1",0,0,1],
+    ["w2",0,1,256],
+    ["w2",1,1,384],
+    ["m1",0,0,2],
+    ["ev",0,0,0],
+    ["w2",0,2,512],
+    ["w2",1,2,0],
+    ["m1",1,0,0],
     ["yI",0,0,512],
-    ["wI",0,1,512],
-    ["m1",1,1],
+    ["wI",0,0,512],
     ["ev",1,0,0],
-    ["wI",0,0,384],
-    ["m1",2,0],
-    ["yI",1,0,384],
-    ["ev",1,1,0],
-    ["wI",1,0,512],
-    ["m1",2,1],
-    ["wI",1,1,512],
+    ["yI",1,0,512],
+    ["m1",2,0,0],
+    ["wI",0,1,512],
+    ["m1",1,1,0],
     ["ev",2,0,0],
-    ["wI",2,1,0],
-    ["yI",2,0,384],
-    ["ev",2,1,0],
-    ["m2p",0,1,0],
-    ["wI",2,0,512],
-    ["m2p",0,1,1],
-    ["yI",2,1,256],
-    ["m2p",0,1,2],
-    ["o",1,1,0],
-    ["o",3,1,0],
-    ["yI",0,1,0],
-    ["yI",1,1,128],
+    ["m1",0,1,1],
+    ["m1",0,1,2],
+    ["wI",1,0,512],
+    ["ev",1,1,0],
+    ["yI",2,0,512],
+    ["wI",2,0,320],
+    ["ev",0,1,0],
+    ["m1",2,1,0],
     ["m2p",0,0,0],
     ["m2p",0,0,1],
+    ["wI",1,1,0],
+    ["wI",2,1,256],
+    ["ev",2,1,0],
     ["m2p",0,0,2],
-    ["o",0,1,0],
-    ["o",2,1,0],
-    ["m2p",1,0,0],
+    ["o",1,0],
+    ["yI",0,1,128],
+    ["o",2,0],
+    ["o",0,0],
+    ["yI",1,1,512],
+    ["o",3,0],
+    ["yI",2,1,0],
+    ["m2p",0,1,0],
+    ["m2p",0,1,1],
+    ["m2p",0,1,2],
+    ["o",1,1],
     ["wI",0,2,0],
-    ["o",2,0,0],
+    ["o",3,1],
+    ["m2p",1,0,0],
     ["m2p",1,0,1],
     ["m2p",1,0,2],
-    ["o",3,0,0],
-    ["o",0,0,0],
-    ["o",1,0,0],
-    ["o",5,0,0],
-    ["m2p",1,1,0],
-    ["o",7,0,0],
+    ["o",0,1],
+    ["o",2,1],
     ["wI",1,2,0],
+    ["m2p",1,1,0],
+    ["o",4,0],
+    ["o",5,0],
+    ["o",6,0],
+    ["o",7,0],
     ["m2p",1,1,1],
     ["m2p",1,1,2],
-    ["o",4,0,0],
-    ["o",6,0,0],
-    ["o",4,1,0],
-    ["wI",2,2,128],
-    ["m2p",1,2,0],
-    ["f"],
-    ["o",6,1,0],
-    ["m2p",1,2,1],
-    ["o",5,1,0],
-    ["m2p",1,2,2],
-    ["o",7,1,0],
     ["m2p",0,2,0],
-    ["o",4,2,0],
-    ["o",7,2,0],
-    ["o",5,2,0],
-    ["o",6,2,0],
+    ["wI",2,2,0],
     ["m2p",0,2,1],
+    ["o",7,1],
+    ["o",4,1],
+    ["f"],
+    ["o",6,1],
     ["m2p",0,2,2],
-    ["o",0,2,0],
-    ["o",1,2,0],
-    ["o",3,2,0],
-    ["o",2,2,0]]
+    ["o",5,1],
+    ["o",2,2],
+    ["o",0,2],
+    ["m2p",1,2,0],
+    ["o",3,2],
+    ["m2p",1,2,1],
+    ["m2p",1,2,2],
+    ["o",1,2],
+    ["o",4,2],
+    ["o",6,2],
+    ["o",7,2],
+    ["o",5,2]]
 
 
 def tile_mixed_hessian_jacobian_e3_kernel(tc, g_words, g_scales, w2, d, wx, wu, lx, lu, q_x, q_u):
@@ -100,13 +102,13 @@ def tile_mixed_hessian_jacobian_e3_kernel(tc, g_words, g_scales, w2, d, wx, wu, 
     with ExitStack() as ctx:
         ctx.enter_context(tc.manual_schedule())
         keep = ctx.enter_context(tc.tile_pool(name="keep", bufs=1))
-        ipool = ctx.enter_context(tc.tile_pool(name="ipool", bufs=8))
-        ypool = ctx.enter_context(tc.tile_pool(name="ypool", bufs=6))
-        opool = ctx.enter_context(tc.tile_pool(name="opool", bufs=8))
+        ipool = ctx.enter_context(tc.tile_pool(name="ipool", bufs=6))
+        ypool = ctx.enter_context(tc.tile_pool(name="ypool", bufs=5))
+        opool = ctx.enter_context(tc.tile_pool(name="opool", bufs=14))
         psum = ctx.enter_context(tc.psum_pool(name="psum", bufs=8))
 
         g_sc = keep.tile([P, 2, NP], U8, align_bytes=64, name="g_sc")
-        nc.gpsimd.memset(g_sc[:].rearrange("p g n -> p (g n)").bitcast(I32), 0)
+        nc.vector.memset(g_sc[:].rearrange("p g n -> p (g n)").bitcast(I32), 0)
         d_raw = keep.tile([P, 3, 4], BF16, align_bytes=64, name="d_raw")
         nc.scalar.dma_start(out=d_raw[:], in_=d.rearrange("(h p t) -> p h t", p=P, t=4))
         d_col = keep.tile([P, 12], F32, align_bytes=64, name="d_col")
@@ -125,20 +127,22 @@ def tile_mixed_hessian_jacobian_e3_kernel(tc, g_words, g_scales, w2, d, wx, wu, 
             src = g_words.rearrange("g p n t -> p g (n t)")[:, :, 2048 * ph : 2048 * (ph + 1)]
             nc.sync.dma_start(out=g_cod[ph][:].bitcast(I32), in_=src.bitcast(I32))
 
-        for g in range(2):
-            for half in range(2):
-                load_w2(g, 0, 256 * half, 256 * (half + 1))
+        def load_gg(g):
+            src = g_words[g].rearrange("p n t -> p (n t)")[:, 0:2048]
+            nc.sync.dma_start(out=g_cod[0][:, g, :].bitcast(I32), in_=src.bitcast(I32))
+
         for q in range(4):
-            nc.sync.dma_start(
+            nc.scalar.dma_start(
                 out=g_sc[32 * q : 32 * q + 4, :, :].bitcast(I32),
                 in_=g_scales[:, 4 * q : 4 * q + 4, :].rearrange("g r n -> r g n").bitcast(I32),
             )
-        load_g(0)
-        load_w2(0, 1, 0, 512)
-        load_w2(1, 1, 0, 512)
+        for g in range(2):
+            load_w2(g, 0, 0, 512)
+            load_gg(g)
+        for hc in (1, 2):
+            for g in range(2):
+                load_w2(g, hc, 0, 512)
         load_g(1)
-        load_w2(0, 2, 0, 512)
-        load_w2(1, 2, 0, 512)
         wx_raw = []
         wu_raw = []
         for hc in range(3):
@@ -213,17 +217,19 @@ def tile_mixed_hessian_jacobian_e3_kernel(tc, g_words, g_scales, w2, d, wx, wu, 
             kind = step[0]
             if kind == "w2":
                 g, hc, v = step[1:]
-                unit(("w2", g, hc), w2_raw[g, hc], v, inter_perm, E4, (0, 256, 512) if hc == 0 else (0, 512))
+                unit(("w2", g, hc), w2_raw[g, hc], v, inter_perm, E4)
             elif kind == "wI":
                 hc, c, v = step[1:]
                 src = wx_raw[hc][:, :, 512 * c : 512 * (c + 1)] if c < 2 else wu_raw[hc][:]
                 unit(("wx", hc, c), src, v, inter, E4)
             elif kind == "m1":
-                hc, ph = step[1:]
+                hc, ph, part = step[1:]
+                passes = (0, 1) if part == 0 else (part - 1,)
                 for t in range(4):
-                    acc = psum.tile([P, 512], F32, name="acc")
-                    acc1[hc, ph, t] = acc
-                    for g in range(2):
+                    if passes[0] == 0:
+                        acc1[hc, ph, t] = psum.tile([P, 512], F32, name="acc")
+                    acc = acc1[hc, ph, t]
+                    for g in passes:
                         nc.tensor.matmul_mx(
                             out=acc[:],
                             lhsT=codes["w2", g, hc][:, 128 * t : 128 * (t + 1)].bitcast(E4),

@@ -17,84 +17,93 @@ NX, NU, NP, H = 1024, 512, 1024, 1536
 P = 128
 FLOPS = 2 * NP * NX * H + 2 * NP * H * (NX + NU)
 
-PLAN = [["w2",0,0,128],
-    ["w2",1,0,512],
+PLAN = [["w2",0,0,320],
+    ["f"],
+    ["w2",1,0,320],
+    ["f"],
     ["m1",0,0,1],
-    ["w2",0,1,256],
-    ["w2",1,1,384],
-    ["m1",0,0,2],
-    ["ev",0,0,0],
+    ["w2",0,1,320],
+    ["w2",1,1,512],
+    ["f"],
     ["w2",0,2,512],
-    ["w2",1,2,0],
+    ["w2",1,2,512],
+    ["m1",0,0,2],
     ["m1",1,0,0],
-    ["yI",0,0,512],
+    ["ev",0,0,0],
+    ["f"],
+    ["yI",0,0,0],
     ["wI",0,0,512],
     ["ev",1,0,0],
-    ["yI",1,0,512],
+    ["f"],
     ["m1",2,0,0],
-    ["wI",0,1,512],
-    ["m1",1,1,0],
+    ["yI",1,0,0],
     ["ev",2,0,0],
-    ["m1",0,1,1],
-    ["m1",0,1,2],
-    ["wI",1,0,512],
-    ["ev",1,1,0],
-    ["yI",2,0,512],
-    ["wI",2,0,320],
-    ["ev",0,1,0],
+    ["f"],
     ["m1",2,1,0],
-    ["m2p",0,0,0],
-    ["m2p",0,0,1],
-    ["wI",1,1,0],
-    ["wI",2,1,256],
+    ["m1",0,1,1],
+    ["wI",0,1,512],
+    ["wI",1,0,512],
+    ["wI",2,0,512],
     ["ev",2,1,0],
+    ["m1",0,1,2],
+    ["yI",2,0,512],
+    ["ev",0,1,0],
+    ["wI",1,1,512],
+    ["m1",1,1,0],
+    ["m2p",0,0,0],
+    ["yI",0,1,512],
+    ["m2p",0,0,1],
+    ["f"],
     ["m2p",0,0,2],
-    ["o",1,0],
-    ["yI",0,1,128],
-    ["o",2,0],
+    ["ev",1,1,0],
     ["o",0,0],
-    ["yI",1,1,512],
+    ["wI",2,1,0],
+    ["o",1,0],
+    ["yI",1,1,0],
+    ["m2p",0,1,0],
+    ["o",2,0],
     ["o",3,0],
     ["yI",2,1,0],
-    ["m2p",0,1,0],
     ["m2p",0,1,1],
     ["m2p",0,1,2],
+    ["o",0,1],
     ["o",1,1],
     ["wI",0,2,0],
+    ["o",2,1],
     ["o",3,1],
+    ["m2p",1,1,0],
+    ["m2p",1,1,1],
+    ["m2p",1,1,2],
+    ["o",4,1],
+    ["wI",1,2,0],
+    ["o",5,1],
+    ["o",6,1],
+    ["o",7,1],
     ["m2p",1,0,0],
     ["m2p",1,0,1],
     ["m2p",1,0,2],
-    ["o",0,1],
-    ["o",2,1],
-    ["wI",1,2,0],
-    ["m2p",1,1,0],
+    ["wI",2,2,0],
     ["o",4,0],
+    ["m2p",0,2,0],
     ["o",5,0],
     ["o",6,0],
-    ["o",7,0],
-    ["m2p",1,1,1],
-    ["m2p",1,1,2],
-    ["m2p",0,2,0],
-    ["wI",2,2,0],
-    ["m2p",0,2,1],
-    ["o",7,1],
-    ["o",4,1],
     ["f"],
-    ["o",6,1],
+    ["m2p",0,2,1],
     ["m2p",0,2,2],
-    ["o",5,1],
-    ["o",2,2],
+    ["o",7,0],
+    ["m2g",4,2],
+    ["m2g",5,2],
     ["o",0,2],
-    ["m2p",1,2,0],
-    ["o",3,2],
-    ["m2p",1,2,1],
-    ["m2p",1,2,2],
     ["o",1,2],
+    ["o",2,2],
+    ["o",3,2],
+    ["m2g",6,2],
+    ["m2g",7,2],
     ["o",4,2],
+    ["o",5,2],
+    ["f"],
     ["o",6,2],
-    ["o",7,2],
-    ["o",5,2]]
+    ["o",7,2]]
 
 
 def tile_mixed_hessian_jacobian_e3_kernel(tc, g_words, g_scales, w2, d, wx, wu, lx, lu, q_x, q_u):
@@ -253,9 +262,15 @@ def tile_mixed_hessian_jacobian_e3_kernel(tc, g_words, g_scales, w2, d, wx, wu, 
             elif kind == "yI":
                 hc, ph, v = step[1:]
                 unit(("y", hc, ph), ytiles[hc, ph], v, inter, E5)
-            elif kind == "m2p":
-                ph, c, hc = step[1:]
-                for pt in range(4 * ph, 4 * ph + 4):
+            elif kind == "m2p" or kind == "m2g":
+                if kind == "m2p":
+                    ph, c = step[1:3]
+                    todo = [(pt, step[3]) for pt in range(4 * ph, 4 * ph + 4)]
+                else:
+                    c = step[2]
+                    ph = step[1] // 4
+                    todo = [(step[1], hc) for hc in range(3)]
+                for pt, hc in todo:
                     if hc == 0:
                         acc2[pt, c] = psum.tile([P, 512], F32, name="acc")
                     cols = slice(128 * (pt % 4), 128 * (pt % 4 + 1))

from contextlib import ExitStack

import concourse.mybir as mybir

F32 = mybir.dt.float32
BF16 = mybir.dt.bfloat16
I32 = mybir.dt.int32
U32 = mybir.dt.uint32
U8 = mybir.dt.uint8
E4 = mybir.dt.float8_e4m3fn_x4
E5 = mybir.dt.float8_e5m2_x4
COPY = mybir.ActivationFunctionType.Copy
ADD = mybir.AluOpType.add
MULT = mybir.AluOpType.mult

NX, NU, NP, H = 1024, 512, 1024, 1536
P = 128
FLOPS = 2 * NP * NX * H + 2 * NP * H * (NX + NU)

PLAN = [["w2",0,0,320],
    ["f"],
    ["w2",1,0,320],
    ["f"],
    ["m1",0,0,1],
    ["w2",0,1,320],
    ["w2",1,1,512],
    ["f"],
    ["w2",0,2,512],
    ["w2",1,2,512],
    ["m1",0,0,2],
    ["m1",1,0,0],
    ["ev",0,0,0],
    ["f"],
    ["yI",0,0,0],
    ["wI",0,0,512],
    ["ev",1,0,0],
    ["f"],
    ["m1",2,0,0],
    ["yI",1,0,0],
    ["ev",2,0,0],
    ["f"],
    ["m1",2,1,0],
    ["m1",0,1,1],
    ["wI",0,1,512],
    ["wI",1,0,512],
    ["wI",2,0,512],
    ["ev",2,1,0],
    ["m1",0,1,2],
    ["yI",2,0,512],
    ["ev",0,1,0],
    ["wI",1,1,512],
    ["m1",1,1,0],
    ["m2p",0,0,0],
    ["yI",0,1,512],
    ["m2p",0,0,1],
    ["f"],
    ["m2p",0,0,2],
    ["ev",1,1,0],
    ["o",0,0],
    ["wI",2,1,0],
    ["o",1,0],
    ["yI",1,1,0],
    ["m2p",0,1,0],
    ["o",2,0],
    ["o",3,0],
    ["yI",2,1,0],
    ["m2p",0,1,1],
    ["m2p",0,1,2],
    ["o",0,1],
    ["o",1,1],
    ["wI",0,2,0],
    ["o",2,1],
    ["o",3,1],
    ["m2p",1,1,0],
    ["m2p",1,1,1],
    ["m2p",1,1,2],
    ["o",4,1],
    ["wI",1,2,0],
    ["o",5,1],
    ["o",6,1],
    ["o",7,1],
    ["m2p",1,0,0],
    ["m2p",1,0,1],
    ["m2p",1,0,2],
    ["wI",2,2,0],
    ["o",4,0],
    ["m2p",0,2,0],
    ["o",5,0],
    ["o",6,0],
    ["f"],
    ["m2p",0,2,1],
    ["m2p",0,2,2],
    ["o",7,0],
    ["m2g",4,2],
    ["m2g",5,2],
    ["o",0,2],
    ["o",1,2],
    ["o",2,2],
    ["o",3,2],
    ["m2g",6,2],
    ["m2g",7,2],
    ["o",4,2],
    ["o",5,2],
    ["f"],
    ["o",6,2],
    ["o",7,2]]


def tile_mixed_hessian_jacobian_e3_kernel(tc, g_words, g_scales, w2, d, wx, wu, lx, lu, q_x, q_u):
    nc = tc.nc
    with ExitStack() as ctx:
        ctx.enter_context(tc.manual_schedule())
        keep = ctx.enter_context(tc.tile_pool(name="keep", bufs=1))
        ipool = ctx.enter_context(tc.tile_pool(name="ipool", bufs=6))
        ypool = ctx.enter_context(tc.tile_pool(name="ypool", bufs=5))
        opool = ctx.enter_context(tc.tile_pool(name="opool", bufs=14))
        psum = ctx.enter_context(tc.psum_pool(name="psum", bufs=8))

        g_sc = keep.tile([P, 2, NP], U8, align_bytes=64, name="g_sc")
        nc.vector.memset(g_sc[:].rearrange("p g n -> p (g n)").bitcast(I32), 0)
        d_raw = keep.tile([P, 3, 4], BF16, align_bytes=64, name="d_raw")
        nc.scalar.dma_start(out=d_raw[:], in_=d.rearrange("(h p t) -> p h t", p=P, t=4))
        d_col = keep.tile([P, 12], F32, align_bytes=64, name="d_col")

        w2_raw = {}
        for hc in range(3):
            for g in range(2):
                w2_raw[g, hc] = keep.tile([P, 4, 512], BF16, align_bytes=64, name="w2r%d%d" % (g, hc))
        g_cod = [keep.tile([P, 2, 512], U32, align_bytes=64, name="gc%d" % ph) for ph in range(2)]

        def load_w2(g, hc, a, b):
            src = w2[512 * g : 512 * (g + 1), 512 * hc + a : 512 * hc + b]
            nc.sync.dma_start(out=w2_raw[g, hc][:, :, a:b], in_=src.rearrange("(p j) c -> p j c", j=4))

        def load_g(ph):
            src = g_words.rearrange("g p n t -> p g (n t)")[:, :, 2048 * ph : 2048 * (ph + 1)]
            nc.sync.dma_start(out=g_cod[ph][:].bitcast(I32), in_=src.bitcast(I32))

        def load_gg(g):
            src = g_words[g].rearrange("p n t -> p (n t)")[:, 0:2048]
            nc.sync.dma_start(out=g_cod[0][:, g, :].bitcast(I32), in_=src.bitcast(I32))

        for q in range(4):
            nc.scalar.dma_start(
                out=g_sc[32 * q : 32 * q + 4, :, :].bitcast(I32),
                in_=g_scales[:, 4 * q : 4 * q + 4, :].rearrange("g r n -> r g n").bitcast(I32),
            )
        for g in range(2):
            load_w2(g, 0, 0, 512)
            load_gg(g)
        for hc in (1, 2):
            for g in range(2):
                load_w2(g, hc, 0, 512)
        load_g(1)
        wx_raw = []
        wu_raw = []
        for hc in range(3):
            t = keep.tile([P, 4, NX], BF16, align_bytes=64, name="wxr%d" % hc)
            nc.sync.dma_start(out=t[:], in_=wx[512 * hc : 512 * (hc + 1), :].rearrange("(p j) c -> p j c", j=4))
            wx_raw.append(t)
        lxt = []
        for ph in range(2):
            lxt.append(keep.tile([P, 4, NX], BF16, align_bytes=64, name="lx%d" % ph))
        lut = keep.tile([P, 8, NU], BF16, align_bytes=64, name="lut")

        def load_lx(ph):
            nc.sync.dma_start(out=lxt[ph][:], in_=lx[512 * ph : 512 * (ph + 1), :].rearrange("(a p) n -> p a n", p=P))

        load_lx(0)
        for hc in range(3):
            t = keep.tile([P, 4, NU], BF16, align_bytes=64, name="wur%d" % hc)
            nc.sync.dma_start(out=t[:], in_=wu[512 * hc : 512 * (hc + 1), :].rearrange("(p j) c -> p j c", j=4))
            wu_raw.append(t)
        load_lx(1)
        nc.sync.dma_start(out=lut[:], in_=lu.rearrange("(a p) n -> p a n", p=P))

        nc.scalar.activation(out=d_col[:], in_=d_raw[:].rearrange("p h t -> p (h t)"), func=COPY)

        codes = {}
        planes = {}
        pending = []

        def flush():
            while pending:
                key, tile_in, fmt = pending.pop(0)
                c = keep.tile([P, 512], U32, align_bytes=64, name="c" + "".join(str(k) for k in key))
                s = keep.tile([P, 512], U8, align_bytes=64, name="s" + "".join(str(k) for k in key))
                nc.vector.quantize_mx(out=c[:].bitcast(fmt), scales=s[:], in_=tile_in[:])
                codes[key] = c
                planes[key] = s

        def inter(dst, src, a, b, on_v):
            o = dst[:, 4 * a : 4 * b].rearrange("p (c i t) -> p c t i", i=4, t=4)
            i = src[:, :, a:b].rearrange("p t (c i) -> p c t i", i=4)
            if on_v:
                nc.vector.tensor_copy(out=o, in_=i)
            else:
                nc.scalar.copy(out=o, in_=i)

        def inter_perm(dst, src, a, b, on_v):
            o = dst[:].rearrange("p (t m j) -> p m j t", t=4, j=4)[:, a // 4 : b // 4]
            i = src[:, :, a:b].rearrange("p j (m t) -> p m j t", t=4)
            if on_v:
                nc.vector.tensor_copy(out=o, in_=i)
            else:
                nc.scalar.copy(out=o, in_=i)

        def unit(key, src, v, fn, fmt, cuts=(0, 512)):
            dst = ipool.tile([P, 2048], BF16, align_bytes=64, name="inter")
            first = True
            for a, b in zip(cuts[:-1], cuts[1:]):
                m = a + v * (b - a) // 512
                if m > a:
                    fn(dst, src, a, m, True)
                if first:
                    flush()
                    first = False
                if m < b:
                    fn(dst, src, m, b, False)
            pending.append((key, dst, fmt))

        acc1 = {}
        acc2 = {}
        ytiles = {}
        for step in PLAN:
            kind = step[0]
            if kind == "w2":
                g, hc, v = step[1:]
                unit(("w2", g, hc), w2_raw[g, hc], v, inter_perm, E4)
            elif kind == "wI":
                hc, c, v = step[1:]
                src = wx_raw[hc][:, :, 512 * c : 512 * (c + 1)] if c < 2 else wu_raw[hc][:]
                unit(("wx", hc, c), src, v, inter, E4)
            elif kind == "m1":
                hc, ph, part = step[1:]
                passes = (0, 1) if part == 0 else (part - 1,)
                for t in range(4):
                    if passes[0] == 0:
                        acc1[hc, ph, t] = psum.tile([P, 512], F32, name="acc")
                    acc = acc1[hc, ph, t]
                    for g in passes:
                        nc.tensor.matmul_mx(
                            out=acc[:],
                            lhsT=codes["w2", g, hc][:, 128 * t : 128 * (t + 1)].bitcast(E4),
                            lhsT_scale=planes["w2", g, hc][:, 128 * t : 128 * (t + 1)],
                            rhs=g_cod[ph][:, g, :].bitcast(E5),
                            rhs_scale=g_sc[:, g, 512 * ph : 512 * (ph + 1)],
                            start=(g == 0),
                            stop=(g == 1),
                        )
            elif kind == "ev":
                hc, ph, nv = step[1:]
                y = ypool.tile([P, 4, 512], BF16, align_bytes=64, name="y")
                ytiles[hc, ph] = y
                for t in range(4):
                    dc = d_col[:, 4 * hc + t : 4 * hc + t + 1]
                    acc = acc1[hc, ph, t]
                    if t >= 4 - nv:
                        nc.vector.tensor_scalar(out=y[:, t, :], in0=acc[:], scalar1=dc, scalar2=None, op0=MULT)
                    else:
                        nc.scalar.activation(out=y[:, t, :], in_=acc[:], func=COPY, scale=dc)
            elif kind == "yI":
                hc, ph, v = step[1:]
                unit(("y", hc, ph), ytiles[hc, ph], v, inter, E5)
            elif kind == "m2p" or kind == "m2g":
                if kind == "m2p":
                    ph, c = step[1:3]
                    todo = [(pt, step[3]) for pt in range(4 * ph, 4 * ph + 4)]
                else:
                    c = step[2]
                    ph = step[1] // 4
                    todo = [(step[1], hc) for hc in range(3)]
                for pt, hc in todo:
                    if hc == 0:
                        acc2[pt, c] = psum.tile([P, 512], F32, name="acc")
                    cols = slice(128 * (pt % 4), 128 * (pt % 4 + 1))
                    nc.tensor.matmul_mx(
                        out=acc2[pt, c][:],
                        lhsT=codes["y", hc, ph][:, cols].bitcast(E5),
                        lhsT_scale=planes["y", hc, ph][:, cols],
                        rhs=codes["wx", hc, c][:].bitcast(E4),
                        rhs_scale=planes["wx", hc, c][:],
                        start=(hc == 0),
                        stop=(hc == 2),
                    )
            elif kind == "o":
                pt, c = step[1:3]
                o = opool.tile([P, 512], F32, align_bytes=64, name="o")
                add = lxt[pt // 4][:, pt % 4, 512 * c : 512 * (c + 1)] if c < 2 else lut[:, pt, :]
                nc.vector.tensor_tensor(out=o[:], in0=acc2[pt, c][:], in1=add, op=ADD)
                rows = slice(P * pt, P * (pt + 1))
                dst = q_x[rows, 512 * c : 512 * (c + 1)] if c < 2 else q_u[rows, :]
                nc.sync.dma_start(out=dst, in_=o[:])
            else:
                flush()
